import numpy as np
CORES = [2,10,18,26,34,42,50,58,66,74,82,90,98,106,114,122]
N = 16
WIDTHS = [512,512,128,128,128,128,512,512,256,25,512,128,256,512,512,25]
XW = 512
def setup_inputs(rng):
    return {"x": rng.standard_normal((N, 128, XW), dtype=np.float32)}
def reference(x):
    g = np.concatenate([x[r][:, :WIDTHS[r]] for r in range(N)], axis=1)
    return {"y": np.broadcast_to(g, (N,) + g.shape)}

@@ -1,0 +1,361 @@
+from concourse.bass import DstId, RemoteDMATransfer
+
+WID = [512, 512, 128, 128, 128, 128, 512, 512, 256, 25, 512, 128, 256, 512, 512, 25]
+CW = 128
+NCELL = sum(w // CW for w in WID if w % CW == 0)
+NGROUP = sum((1 if w % CW or w == CW else 2) for w in WID)
+
+OPT = {"nrelay": 0, "lag": 2, "split": True, "rankfwd": 0, "hm": 1, "order": "rot"}
+
+SCRATCH = {"cb": ("dram", [NCELL, 128, CW], "float32")}
+for rr, ww in enumerate(WID):
+    if ww % CW:
+        SCRATCH["t%d" % rr] = ("dram", [128, ww], "float32")
+SEMAPHORES = ["ld", "dl", "sent", "ssy", "ssc"] + ["a%d" % i for i in range(NGROUP)]
+
+CACHE = {}
+
+
+def eng(lo, cnt):
+    return ((1 << cnt) - 1) << lo
+
+
+def list_schedule(jobs, lag):
+    rem_out, rem_in = {}, {}
+    for j in jobs:
+        rem_out[(j["src"], j["die"])] = rem_out.get((j["src"], j["die"]), 0) + j["ln"]
+        rem_in[(j["dst"], j["die"])] = rem_in.get((j["dst"], j["die"]), 0) + j["ln"]
+    outf, inf = {}, {}
+    todo = list(range(len(jobs)))
+    t = 0
+    while todo:
+        ports = sorted(set((jobs[i]["src"], jobs[i]["die"]) for i in todo), key=lambda p: (-rem_out[p], p))
+        for p in ports:
+            if outf.get(p, 0) > t:
+                continue
+            best, bkey = None, None
+            for i in todo:
+                j = jobs[i]
+                if (j["src"], j["die"]) != p or j["avail"] is None or j["avail"] > t:
+                    continue
+                q = (j["dst"], j["die"])
+                if inf.get(q, 0) > t:
+                    continue
+                key = (-len(j["kids"]), -rem_in[q], i)
+                if best is None or key < bkey:
+                    best, bkey = i, key
+            if best is None:
+                continue
+            j = jobs[best]
+            q = (j["dst"], j["die"])
+            j["start"] = t
+            outf[p] = t + j["ln"]
+            inf[q] = t + j["ln"]
+            rem_out[p] -= j["ln"]
+            rem_in[q] -= j["ln"]
+            for k in j["kids"]:
+                jobs[k]["avail"] = t + j["ln"] + lag
+            todo.remove(best)
+        t += 1
+
+
+def make_plan(wid, cores, topo, opt):
+    n = len(wid)
+    off = [sum(wid[:r]) for r in range(n)]
+    chip_of = [topo.chip(c) for c in cores]
+    rcore = dict((chip_of[r], cores[r]) for r in range(n))
+    lag = opt["lag"]
+
+    cells, groups = [], []
+    ncell = {}
+    for r, w in enumerate(wid):
+        if w % CW:
+            ncell[chip_of[r]] = 0
+            groups.append({"rank": r, "cells": [], "die": None})
+            continue
+        k = w // CW
+        rows = 128 // k
+        ids = []
+        for i in range(k):
+            ids.append(len(cells))
+            cells.append((r, i * rows, (i + 1) * rows))
+        ncell[chip_of[r]] = k
+        if k == 1:
+            groups.append({"rank": r, "cells": ids, "die": None})
+        else:
+            groups.append({"rank": r, "cells": ids[:k // 2], "die": 1})
+            groups.append({"rank": r, "cells": ids[k // 2:], "die": 0})
+    for i, gr in enumerate(groups):
+        gr["gid"] = i
+        gr["chip"] = chip_of[gr["rank"]]
+
+    jobs = []
+    outl, inl = {}, {}
+
+    def add_job(gr, src, dst, die, parent):
+        j = {"g": gr["gid"], "src": src, "dst": dst, "die": die, "ln": len(gr["cells"]), "kids": [],
+             "avail": 0 if parent is None else None, "parent": parent, "start": None}
+        jobs.append(j)
+        outl[(src, die)] = outl.get((src, die), 0) + j["ln"]
+        inl[(dst, die)] = inl.get((dst, die), 0) + j["ln"]
+        if parent is not None:
+            jobs[parent]["kids"].append(len(jobs) - 1)
+        return len(jobs) - 1
+
+    for par in (0, 1):
+        mem = sorted(c for c in chip_of if c % 2 == par)
+        load = dict((c, (len(mem) - 1) * ncell[c]) for c in mem)
+        for i, a in enumerate(mem):
+            rot = [mem[(i + s) % len(mem)] for s in range(1, len(mem))]
+            mine = [gr for gr in groups if gr["chip"] == a and gr["die"] is not None]
+            if ncell[a] == 4 and opt["nrelay"]:
+                via = sorted((c for c in mem if ncell[c] < 4), key=lambda c: (load[c], c))[:opt["nrelay"]]
+                rest = [d for d in rot if d not in via]
+                far = rest[len(rest) - len(via):]
+                for gr in mine:
+                    for d in rest[:len(rest) - len(via)]:
+                        add_job(gr, a, d, gr["die"], None)
+                    for v, d in zip(via, far):
+                        p = add_job(gr, a, v, gr["die"], None)
+                        add_job(gr, v, d, gr["die"], p)
+                for v in via:
+                    load[v] += ncell[a]
+            else:
+                for gr in mine:
+                    for d in rot:
+                        add_job(gr, a, d, gr["die"], None)
+        for i, a in enumerate(mem):
+            for gr in groups:
+                if gr["chip"] == a and gr["die"] is None and gr["cells"]:
+                    for s in range(1, len(mem)):
+                        d = mem[(i + s) % len(mem)]
+                        cost = [max(outl.get((a, e), 0), inl.get((d, e), 0)) * 100 + outl.get((a, e), 0)
+                                + inl.get((d, e), 0) for e in (0, 1)]
+                        add_job(gr, a, d, 1 if cost[1] < cost[0] else 0, None)
+    list_schedule(jobs, lag)
+    if opt["order"] == "rot":
+        for j in jobs:
+            if j["parent"] is None:
+                j["start"] = (((j["dst"] - j["src"]) // 2) % 8 - 1) * 2
+        for j in jobs:
+            if j["parent"] is not None:
+                j["start"] = jobs[j["parent"]]["start"] + j["ln"] + lag
+
+    prog = {}
+    arrive = {}
+    sent = {}
+
+    def P(core):
+        if core not in prog:
+            prog[core] = {"g": [], "sync": [], "scalar": []}
+        return prog[core]
+
+    def call(core, transfers, lsem):
+        for spec, dsts, mask, gid in transfers:
+            cnt = bin(mask).count("1")
+            for d in dsts:
+                arrive[(d, gid)] = arrive.get((d, gid), 0) + cnt
+            sent[(core, lsem)] = sent.get((core, lsem), 0) + cnt
+        P(core)["g"].append(("call", transfers, lsem))
+
+    est = {}
+
+    hsend = {}
+    for ji, j in enumerate(jobs):
+        j["idx"] = ji
+    for c in chip_of:
+        for die in (0, 1):
+            h = [8 * c + (0 if die else 4), 8 * c + (1 if die else 5)]
+            mine = sorted((j for j in jobs if j["src"] == c and j["die"] == die and j["parent"] is None),
+                          key=lambda j: (j["start"], j["idx"]))
+            alt = 0
+            for j in mine:
+                cs = groups[j["g"]]["cells"]
+                if len(cs) == 2:
+                    for hh, cell in zip(h, cs):
+                        hsend.setdefault(hh, []).append((cell, j))
+                else:
+                    hsend.setdefault(h[alt], []).append((cs[0], j))
+                    alt ^= 1
+
+    node = {}
+    mate_jobs = {}
+    for c in chip_of:
+        arr = sorted((j for j in jobs if j["dst"] == c), key=lambda j: (j["start"] + j["ln"], j["idx"]))
+        L = {1: ncell[c], 0: 0}
+        die_of = {}
+        for j in arr:
+            if j["kids"]:
+                die_of[j["idx"]] = j["die"]
+                L[j["die"]] += j["ln"]
+        for j in sorted((j for j in arr if not j["kids"]), key=lambda j: (-j["ln"], j["start"], j["idx"])):
+            e = 1 if L[1] < L[0] else 0
+            die_of[j["idx"]] = e
+            L[e] += j["ln"]
+        cnt = {6: 0, 7: 0}
+        n3 = 0
+        for j in arr:
+            if die_of[j["idx"]] == 1:
+                k = 3
+                n3 += 1
+                if opt["rankfwd"] and j["ln"] == 1 and not j["kids"] and n3 % opt["rankfwd"] == 0:
+                    k = 2
+            else:
+                k = 6 if cnt[6] <= cnt[7] else 7
+                cnt[k] += j["ln"]
+            node[(c, j["g"])] = 8 * c + k
+            mate_jobs.setdefault((c, die_of[j["idx"]]), []).append(j)
+
+    for r in range(n):
+        c, core, w = chip_of[r], cores[r], wid[r]
+        mate = rcore[c ^ 1]
+        mine = [gr for gr in groups if gr["rank"] == r]
+        if w % CW:
+            gr = mine[0]
+            P(core)["sync"].append(("dma", ("t", r), ("x", 0, 128, w), "ld"))
+            P(core)["g"].append(("wait", "ld", 16))
+            others = [mate] + [cores[q] for q in range(n) if q != r and cores[q] != mate]
+            call(core, [(("t", r), others, eng(0, 8), gr["gid"])], "dl")
+            for q in range(n):
+                if q != r:
+                    est[(chip_of[q], gr["gid"])] = 0.5
+            continue
+        k0 = mine[0]["cells"][0]
+        k = w // CW
+        P(core)["sync"].append(("dma", ("cbr", k0, k0 + k), ("x", 0, 128, w), "ld"))
+        P(core)["g"].append(("wait", "ld", 16))
+        gid_of = {}
+        for gr in mine:
+            for cell in gr["cells"]:
+                gid_of[cell] = gr["gid"]
+        need = []
+        for hh in sorted(hsend):
+            if hh // 8 == c:
+                for cell in sorted(set(cell for cell, j in hsend[hh])):
+                    need.append((cell, hh))
+        per = 16
+        while per * len(need) > 16:
+            per //= 2
+        call(core, [(("cb", cell), [hh], eng(i * per, per), gid_of[cell]) for i, (cell, hh) in enumerate(need)], "dl")
+        per = 8 // k
+        call(core, [(("cb", k0 + i), [mate], eng(i * per, per), gid_of[k0 + i]) for i in range(k)], "sent")
+        for gr in mine:
+            est[(c ^ 1, gr["gid"])] = 0.25 * k
+
+    for hh in sorted(hsend):
+        lst = hsend[hh]
+        seen = []
+        for cell, j in lst:
+            if j["g"] not in seen:
+                seen.append(j["g"])
+        for gid in seen:
+            P(hh)["g"].append(("waitg", gid))
+        if opt["split"]:
+            hm = opt["hm"]
+            for i, (cell, j) in enumerate(lst):
+                call(hh, [(("cb", cell), [node[(j["dst"], j["g"])]], eng((i % hm) * (8 // hm), 8 // hm), j["g"])], "sent")
+        else:
+            for cell in sorted(set(cell for cell, j in lst)):
+                sub = [j for cc, j in lst if cc == cell]
+                call(hh, [(("cb", cell), [node[(j["dst"], j["g"])] for j in sub], eng(0, 8), sub[0]["g"])], "sent")
+
+    acts = {}
+    for (c, die), lst in sorted(mate_jobs.items()):
+        free = ncell[c] if die == 1 else 0
+        for j in sorted(lst, key=lambda j: (j["start"] + j["ln"], j["idx"])):
+            a = j["start"] + j["ln"]
+            free = max(free, a + lag) + j["ln"]
+            est[(c ^ 1, j["g"])] = free
+            est[(c, j["g"])] = a + (lag + 0.5 * j["ln"] if node[(c, j["g"])] != rcore[c] else 0)
+            acts.setdefault(node[(c, j["g"])], []).append(j)
+    for nd in sorted(acts):
+        c = nd // 8
+        for j in sorted(acts[nd], key=lambda j: (j["start"] + j["ln"], j["idx"])):
+            gr = groups[j["g"]]
+            m = len(gr["cells"])
+            per = 8 // m
+            tr = []
+            kid = [node[(jobs[k]["dst"], j["g"])] for k in j["kids"]]
+            if kid:
+                per //= 2
+                for i, cell in enumerate(gr["cells"]):
+                    tr.append((("cb", cell), kid, eng(i * per, per), j["g"]))
+                for i, cell in enumerate(gr["cells"]):
+                    tr.append((("cb", cell), [rcore[c ^ 1]], eng(4 + i * per, per), j["g"]))
+                per *= 2
+            else:
+                for i, cell in enumerate(gr["cells"]):
+                    tr.append((("cb", cell), [rcore[c ^ 1]], eng(i * per, per), j["g"]))
+            if nd != rcore[c]:
+                for i, cell in enumerate(gr["cells"]):
+                    tr.append((("cb", cell), [rcore[c]], eng(8 + i * per, per), j["g"]))
+            P(nd)["g"].append(("waitg", j["g"]))
+            call(nd, tr, "sent")
+
+    for r in range(n):
+        c, core, w = chip_of[r], cores[r], wid[r]
+        pr = P(core)
+        pr["scalar"].append(("wait", "dl", sent[(core, "dl")]))
+        pr["scalar"].append(("dma", ("y", 0, 128, off[r], off[r] + w), ("x", 0, 128, w), "ssc"))
+        cnt = {"sync": 0, "scalar": 1}
+        todo = sorted((gr for gr in groups if gr["rank"] != r), key=lambda gr: (est[(c, gr["gid"])], gr["gid"]))
+        for i, gr in enumerate(todo):
+            q = "sync" if i % 2 == 0 else "scalar"
+            o, ww = off[gr["rank"]], wid[gr["rank"]]
+            pr[q].append(("waitg", gr["gid"]))
+            if gr["cells"]:
+                k0, k1 = gr["cells"][0], gr["cells"][-1]
+                src = ("cb", k0) if k0 == k1 else ("cbr", k0, k1 + 1)
+                pr[q].append(("dma", ("y", cells[k0][1], cells[k1][2], o, o + ww), src, "ssy" if q == "sync" else "ssc"))
+            else:
+                pr[q].append(("dma", ("y", 0, 128, o, o + ww), ("t", gr["rank"]), "ssy" if q == "sync" else "ssc"))
+            cnt[q] += 1
+        pr["sync"].append(("wait", "ssy", 16 * cnt["sync"]))
+        pr["scalar"].append(("wait", "ssc", 16 * cnt["scalar"]))
+
+    for core in prog:
+        if (core, "sent") in sent:
+            prog[core]["g"].append(("wait", "sent", sent[(core, "sent")]))
+        for q in prog[core]:
+            prog[core][q] = [("wait", "a%d" % op[1], arrive[(core, op[1])]) if op[0] == "waitg" else op
+                             for op in prog[core][q]]
+    return {"prog": prog, "jobs": jobs, "groups": groups, "node": node, "est": est}
+
+
+def rank_program(g, core, T, topo):
+    if "plan" not in CACHE:
+        CACHE["plan"] = make_plan(list(T.tables["WIDTHS"]), list(T.cores), topo, OPT)
+    ops = CACHE["plan"]["prog"].get(core)
+    if not ops:
+        return
+
+    def ap(s):
+        if s[0] == "cb":
+            return T.cb[s[1]]
+        if s[0] == "cbr":
+            return T.cb[s[1]:s[2]]
+        if s[0] == "t":
+            return T["t%d" % s[1]][:]
+        if s[0] == "x":
+            return T.x[s[1]:s[2], 0:s[3]]
+        return T.y[s[1]:s[2], s[3]:s[4]]
+
+    for qn, q in (("sync", g.sync), ("scalar", g.scalar), ("g", g)):
+        for op in ops[qn]:
+            if op[0] == "wait":
+                q.wait_ge(T.sem[op[1]], op[2])
+            elif op[0] == "dma":
+                q.dma_start(ap(op[1]), ap(op[2])).then_inc(T.sem[op[3]], 16)
+            else:
+                trs, lsem = op[1], op[2]
+                if len(trs) == 1 and len(trs[0][1]) == 1:
+                    spec, dsts, mask, gid = trs[0]
+                    rid, pid, se = topo.addr(dsts[0])
+                    g.remote_dma(ap(spec), ap(spec), T.sem["a%d" % gid], T.sem[lsem], pid, rid, mask)
+                else:
+                    lst = []
+                    for spec, dsts, mask, gid in trs:
+                        ids = [DstId(rid=topo.addr(d)[0], pnc=topo.addr(d)[1]) for d in dsts]
+                        lst.append(RemoteDMATransfer(dst_ids=ids, dma_engine_mask=mask, remote_sem=T.sem["a%d" % gid],
+                                                     srcs=[ap(spec)], dsts=[ap(spec) for d in dsts], alu_op=0))
+                    g.remote_dma_fused(lst, local_sem=T.sem[lsem])

@@ -5,7 +5,7 @@ CW = 128
 NCELL = sum(w // CW for w in WID if w % CW == 0)
 NGROUP = sum((1 if w % CW or w == CW else 2) for w in WID)
 
-OPT = {"nrelay": 0, "lag": 2, "split": True, "rankfwd": 0, "hm": 1, "order": "rot"}
+OPT = {"nrelay": 2, "lag": 2, "split": True, "hm": 1, "order": "list", "merge": 0}
 
 SCRATCH = {"cb": ("dram", [NCELL, 128, CW], "float32")}
 for rr, ww in enumerate(WID):
@@ -184,28 +184,41 @@ def make_plan(wid, cores, topo, opt):
         arr = sorted((j for j in jobs if j["dst"] == c), key=lambda j: (j["start"] + j["ln"], j["idx"]))
         L = {1: ncell[c], 0: 0}
         die_of = {}
-        for j in arr:
-            if j["kids"]:
-                die_of[j["idx"]] = j["die"]
-                L[j["die"]] += j["ln"]
-        for j in sorted((j for j in arr if not j["kids"]), key=lambda j: (-j["ln"], j["start"], j["idx"])):
-            e = 1 if L[1] < L[0] else 0
-            die_of[j["idx"]] = e
-            L[e] += j["ln"]
+        if opt["merge"]:
+            byr = {}
+            for j in arr:
+                byr.setdefault(groups[j["g"]]["rank"], []).append(j)
+            for rk in sorted(byr, key=lambda rk: (-sum(j["ln"] for j in byr[rk]), byr[rk][0]["start"], rk)):
+                e = 1 if L[1] < L[0] else 0
+                for j in byr[rk]:
+                    die_of[j["idx"]] = e
+                    L[e] += j["ln"]
+        else:
+            for j in arr:
+                if j["kids"]:
+                    die_of[j["idx"]] = j["die"]
+                    L[j["die"]] += j["ln"]
+            for j in sorted((j for j in arr if not j["kids"]), key=lambda j: (-j["ln"], j["start"], j["idx"])):
+                e = 1 if L[1] < L[0] else 0
+                die_of[j["idx"]] = e
+                L[e] += j["ln"]
         cnt = {6: 0, 7: 0}
-        n3 = 0
+        pick = {}
         for j in arr:
-            if die_of[j["idx"]] == 1:
+            rk = groups[j["g"]]["rank"]
+            if opt["merge"] and rk in pick:
+                k = pick[rk]
+            elif die_of[j["idx"]] == 1:
                 k = 3
-                n3 += 1
-                if opt["rankfwd"] and j["ln"] == 1 and not j["kids"] and n3 % opt["rankfwd"] == 0:
-                    k = 2
             else:
                 k = 6 if cnt[6] <= cnt[7] else 7
+            if k in cnt:
                 cnt[k] += j["ln"]
+            pick[rk] = k
             node[(c, j["g"])] = 8 * c + k
             mate_jobs.setdefault((c, die_of[j["idx"]]), []).append(j)
 
+    tiny = {}
     for r in range(n):
         c, core, w = chip_of[r], cores[r], wid[r]
         mate = rcore[c ^ 1]
@@ -214,11 +227,13 @@ def make_plan(wid, cores, topo, opt):
             gr = mine[0]
             P(core)["sync"].append(("dma", ("t", r), ("x", 0, 128, w), "ld"))
             P(core)["g"].append(("wait", "ld", 16))
-            others = [mate] + [cores[q] for q in range(n) if q != r and cores[q] != mate]
-            call(core, [(("t", r), others, eng(0, 8), gr["gid"])], "dl")
-            for q in range(n):
-                if q != r:
-                    est[(chip_of[q], gr["gid"])] = 0.5
+            same = [d for d in chip_of if d != c and d % 2 == c % 2]
+            call(core, [(("t", r), [mate] + [rcore[d] for d in same] + [8 * d + 7 for d in same], eng(0, 8), gr["gid"])], "dl")
+            for d in same:
+                est[(d, gr["gid"])] = 0.5
+                est[(d ^ 1, gr["gid"])] = 3
+                tiny.setdefault(d, []).append(gr)
+            est[(c ^ 1, gr["gid"])] = 0.5
             continue
         k0 = mine[0]["cells"][0]
         k = w // CW
@@ -259,6 +274,12 @@ def make_plan(wid, cores, topo, opt):
                 sub = [j for cc, j in lst if cc == cell]
                 call(hh, [(("cb", cell), [node[(j["dst"], j["g"])] for j in sub], eng(0, 8), sub[0]["g"])], "sent")
 
+    for d in sorted(tiny):
+        per = 8 // len(tiny[d])
+        for gr in tiny[d]:
+            P(8 * d + 7)["g"].append(("waitg", gr["gid"]))
+        call(8 * d + 7, [(("t", gr["rank"]), [rcore[d ^ 1]], eng(i * per, per), gr["gid"]) for i, gr in enumerate(tiny[d])], "sent")
+
     acts = {}
     for (c, die), lst in sorted(mate_jobs.items()):
         free = ncell[c] if die == 1 else 0
@@ -266,30 +287,32 @@ def make_plan(wid, cores, topo, opt):
             a = j["start"] + j["ln"]
             free = max(free, a + lag) + j["ln"]
             est[(c ^ 1, j["g"])] = free
-            est[(c, j["g"])] = a + (lag + 0.5 * j["ln"] if node[(c, j["g"])] != rcore[c] else 0)
+            est[(c, j["g"])] = a + lag + 0.5 * j["ln"]
             acts.setdefault(node[(c, j["g"])], []).append(j)
     for nd in sorted(acts):
         c = nd // 8
+        batches = []
         for j in sorted(acts[nd], key=lambda j: (j["start"] + j["ln"], j["idx"])):
-            gr = groups[j["g"]]
-            m = len(gr["cells"])
-            per = 8 // m
-            tr = []
-            kid = [node[(jobs[k]["dst"], j["g"])] for k in j["kids"]]
-            if kid:
-                per //= 2
-                for i, cell in enumerate(gr["cells"]):
-                    tr.append((("cb", cell), kid, eng(i * per, per), j["g"]))
-                for i, cell in enumerate(gr["cells"]):
-                    tr.append((("cb", cell), [rcore[c ^ 1]], eng(4 + i * per, per), j["g"]))
-                per *= 2
+            if opt["merge"] and batches and groups[batches[-1][0]["g"]]["rank"] == groups[j["g"]]["rank"]:
+                batches[-1].append(j)
             else:
-                for i, cell in enumerate(gr["cells"]):
+                batches.append([j])
+        for bt in batches:
+            cl = [(cell, j) for j in bt for cell in groups[j["g"]]["cells"]]
+            per = 8 // len(cl)
+            tr = []
+            if bt[0]["kids"]:
+                hp = per // 2
+                for i, (cell, j) in enumerate(cl):
+                    tr.append((("cb", cell), [node[(jobs[k]["dst"], j["g"])] for k in j["kids"]], eng(i * hp, hp), j["g"]))
+                    tr.append((("cb", cell), [rcore[c ^ 1]], eng(4 + i * hp, hp), j["g"]))
+            else:
+                for i, (cell, j) in enumerate(cl):
                     tr.append((("cb", cell), [rcore[c ^ 1]], eng(i * per, per), j["g"]))
-            if nd != rcore[c]:
-                for i, cell in enumerate(gr["cells"]):
-                    tr.append((("cb", cell), [rcore[c]], eng(8 + i * per, per), j["g"]))
-            P(nd)["g"].append(("waitg", j["g"]))
+            for i, (cell, j) in enumerate(cl):
+                tr.append((("cb", cell), [rcore[c]], eng(8 + i * per, per), j["g"]))
+            for j in bt:
+                P(nd)["g"].append(("waitg", j["g"]))
             call(nd, tr, "sent")
 
     for r in range(n):
@@ -299,12 +322,25 @@ def make_plan(wid, cores, topo, opt):
         pr["scalar"].append(("dma", ("y", 0, 128, off[r], off[r] + w), ("x", 0, 128, w), "ssc"))
         cnt = {"sync": 0, "scalar": 1}
         todo = sorted((gr for gr in groups if gr["rank"] != r), key=lambda gr: (est[(c, gr["gid"])], gr["gid"]))
-        for i, gr in enumerate(todo):
+        if opt["merge"]:
+            late = {}
+            for gr in todo:
+                late[gr["rank"]] = max(late.get(gr["rank"], 0), est[(c, gr["gid"])])
+            todo = sorted(todo, key=lambda gr: (late[gr["rank"]], gr["gid"]))
+        bts = []
+        for gr in todo:
+            if opt["merge"] and bts and bts[-1][0]["rank"] == gr["rank"]:
+                bts[-1].append(gr)
+            else:
+                bts.append([gr])
+        for i, bt in enumerate(bts):
             q = "sync" if i % 2 == 0 else "scalar"
+            gr = bt[0]
             o, ww = off[gr["rank"]], wid[gr["rank"]]
-            pr[q].append(("waitg", gr["gid"]))
+            for g2 in bt:
+                pr[q].append(("waitg", g2["gid"]))
             if gr["cells"]:
-                k0, k1 = gr["cells"][0], gr["cells"][-1]
+                k0, k1 = bt[0]["cells"][0], bt[-1]["cells"][-1]
                 src = ("cb", k0) if k0 == k1 else ("cbr", k0, k1 + 1)
                 pr[q].append(("dma", ("y", cells[k0][1], cells[k1][2], o, o + ww), src, "ssy" if q == "sync" else "ssc"))
             else:

@@ -5,7 +5,7 @@ CW = 128
 NCELL = sum(w // CW for w in WID if w % CW == 0)
 NGROUP = sum((1 if w % CW or w == CW else 2) for w in WID)
 
-OPT = {"nrelay": 2, "lag": 2, "split": True, "hm": 1, "order": "list", "merge": 0}
+OPT = {"nrelay": 2, "lag": 2}
 
 SCRATCH = {"cb": ("dram", [NCELL, 128, CW], "float32")}
 for rr, ww in enumerate(WID):
@@ -133,13 +133,6 @@ def make_plan(wid, cores, topo, opt):
                                 + inl.get((d, e), 0) for e in (0, 1)]
                         add_job(gr, a, d, 1 if cost[1] < cost[0] else 0, None)
     list_schedule(jobs, lag)
-    if opt["order"] == "rot":
-        for j in jobs:
-            if j["parent"] is None:
-                j["start"] = (((j["dst"] - j["src"]) // 2) % 8 - 1) * 2
-        for j in jobs:
-            if j["parent"] is not None:
-                j["start"] = jobs[j["parent"]]["start"] + j["ln"] + lag
 
     prog = {}
     arrive = {}
@@ -184,37 +177,21 @@ def make_plan(wid, cores, topo, opt):
         arr = sorted((j for j in jobs if j["dst"] == c), key=lambda j: (j["start"] + j["ln"], j["idx"]))
         L = {1: ncell[c], 0: 0}
         die_of = {}
-        if opt["merge"]:
-            byr = {}
-            for j in arr:
-                byr.setdefault(groups[j["g"]]["rank"], []).append(j)
-            for rk in sorted(byr, key=lambda rk: (-sum(j["ln"] for j in byr[rk]), byr[rk][0]["start"], rk)):
-                e = 1 if L[1] < L[0] else 0
-                for j in byr[rk]:
-                    die_of[j["idx"]] = e
-                    L[e] += j["ln"]
-        else:
-            for j in arr:
-                if j["kids"]:
-                    die_of[j["idx"]] = j["die"]
-                    L[j["die"]] += j["ln"]
-            for j in sorted((j for j in arr if not j["kids"]), key=lambda j: (-j["ln"], j["start"], j["idx"])):
-                e = 1 if L[1] < L[0] else 0
-                die_of[j["idx"]] = e
-                L[e] += j["ln"]
-        cnt = {6: 0, 7: 0}
-        pick = {}
         for j in arr:
-            rk = groups[j["g"]]["rank"]
-            if opt["merge"] and rk in pick:
-                k = pick[rk]
-            elif die_of[j["idx"]] == 1:
+            if j["kids"]:
+                die_of[j["idx"]] = j["die"]
+                L[j["die"]] += j["ln"]
+        for j in sorted((j for j in arr if not j["kids"]), key=lambda j: (-j["ln"], j["start"], j["idx"])):
+            e = 1 if L[1] < L[0] else 0
+            die_of[j["idx"]] = e
+            L[e] += j["ln"]
+        cnt = {6: 0, 7: 0}
+        for j in arr:
+            if die_of[j["idx"]] == 1:
                 k = 3
             else:
                 k = 6 if cnt[6] <= cnt[7] else 7
-            if k in cnt:
                 cnt[k] += j["ln"]
-            pick[rk] = k
             node[(c, j["g"])] = 8 * c + k
             mate_jobs.setdefault((c, die_of[j["idx"]]), []).append(j)
 
@@ -265,14 +242,8 @@ def make_plan(wid, cores, topo, opt):
                 seen.append(j["g"])
         for gid in seen:
             P(hh)["g"].append(("waitg", gid))
-        if opt["split"]:
-            hm = opt["hm"]
-            for i, (cell, j) in enumerate(lst):
-                call(hh, [(("cb", cell), [node[(j["dst"], j["g"])]], eng((i % hm) * (8 // hm), 8 // hm), j["g"])], "sent")
-        else:
-            for cell in sorted(set(cell for cell, j in lst)):
-                sub = [j for cc, j in lst if cc == cell]
-                call(hh, [(("cb", cell), [node[(j["dst"], j["g"])] for j in sub], eng(0, 8), sub[0]["g"])], "sent")
+        for cell, j in lst:
+            call(hh, [(("cb", cell), [node[(j["dst"], j["g"])]], eng(0, 8), j["g"])], "sent")
 
     for d in sorted(tiny):
         per = 8 // len(tiny[d])
@@ -291,28 +262,21 @@ def make_plan(wid, cores, topo, opt):
             acts.setdefault(node[(c, j["g"])], []).append(j)
     for nd in sorted(acts):
         c = nd // 8
-        batches = []
         for j in sorted(acts[nd], key=lambda j: (j["start"] + j["ln"], j["idx"])):
-            if opt["merge"] and batches and groups[batches[-1][0]["g"]]["rank"] == groups[j["g"]]["rank"]:
-                batches[-1].append(j)
-            else:
-                batches.append([j])
-        for bt in batches:
-            cl = [(cell, j) for j in bt for cell in groups[j["g"]]["cells"]]
+            cl = groups[j["g"]]["cells"]
             per = 8 // len(cl)
             tr = []
-            if bt[0]["kids"]:
+            if j["kids"]:
                 hp = per // 2
-                for i, (cell, j) in enumerate(cl):
+                for i, cell in enumerate(cl):
                     tr.append((("cb", cell), [node[(jobs[k]["dst"], j["g"])] for k in j["kids"]], eng(i * hp, hp), j["g"]))
                     tr.append((("cb", cell), [rcore[c ^ 1]], eng(4 + i * hp, hp), j["g"]))
             else:
-                for i, (cell, j) in enumerate(cl):
+                for i, cell in enumerate(cl):
                     tr.append((("cb", cell), [rcore[c ^ 1]], eng(i * per, per), j["g"]))
-            for i, (cell, j) in enumerate(cl):
+            for i, cell in enumerate(cl):
                 tr.append((("cb", cell), [rcore[c]], eng(8 + i * per, per), j["g"]))
-            for j in bt:
-                P(nd)["g"].append(("waitg", j["g"]))
+            P(nd)["g"].append(("waitg", j["g"]))
             call(nd, tr, "sent")
 
     for r in range(n):
@@ -322,25 +286,12 @@ def make_plan(wid, cores, topo, opt):
         pr["scalar"].append(("dma", ("y", 0, 128, off[r], off[r] + w), ("x", 0, 128, w), "ssc"))
         cnt = {"sync": 0, "scalar": 1}
         todo = sorted((gr for gr in groups if gr["rank"] != r), key=lambda gr: (est[(c, gr["gid"])], gr["gid"]))
-        if opt["merge"]:
-            late = {}
-            for gr in todo:
-                late[gr["rank"]] = max(late.get(gr["rank"], 0), est[(c, gr["gid"])])
-            todo = sorted(todo, key=lambda gr: (late[gr["rank"]], gr["gid"]))
-        bts = []
-        for gr in todo:
-            if opt["merge"] and bts and bts[-1][0]["rank"] == gr["rank"]:
-                bts[-1].append(gr)
-            else:
-                bts.append([gr])
-        for i, bt in enumerate(bts):
+        for i, gr in enumerate(todo):
             q = "sync" if i % 2 == 0 else "scalar"
-            gr = bt[0]
             o, ww = off[gr["rank"]], wid[gr["rank"]]
-            for g2 in bt:
-                pr[q].append(("waitg", g2["gid"]))
+            pr[q].append(("waitg", gr["gid"]))
             if gr["cells"]:
-                k0, k1 = bt[0]["cells"][0], bt[-1]["cells"][-1]
+                k0, k1 = gr["cells"][0], gr["cells"][-1]
                 src = ("cb", k0) if k0 == k1 else ("cbr", k0, k1 + 1)
                 pr[q].append(("dma", ("y", cells[k0][1], cells[k1][2], o, o + ww), src, "ssy" if q == "sync" else "ssc"))
             else:

from concourse.bass import DstId, RemoteDMATransfer

WID = [512, 512, 128, 128, 128, 128, 512, 512, 256, 25, 512, 128, 256, 512, 512, 25]
CW = 128
NCELL = sum(w // CW for w in WID if w % CW == 0)
NGROUP = sum((1 if w % CW or w == CW else 2) for w in WID)

OPT = {"nrelay": 2, "lag": 2}

SCRATCH = {"cb": ("dram", [NCELL, 128, CW], "float32")}
for rr, ww in enumerate(WID):
    if ww % CW:
        SCRATCH["t%d" % rr] = ("dram", [128, ww], "float32")
SEMAPHORES = ["ld", "dl", "sent", "ssy", "ssc"] + ["a%d" % i for i in range(NGROUP)]

CACHE = {}


def eng(lo, cnt):
    return ((1 << cnt) - 1) << lo


def list_schedule(jobs, lag):
    rem_out, rem_in = {}, {}
    for j in jobs:
        rem_out[(j["src"], j["die"])] = rem_out.get((j["src"], j["die"]), 0) + j["ln"]
        rem_in[(j["dst"], j["die"])] = rem_in.get((j["dst"], j["die"]), 0) + j["ln"]
    outf, inf = {}, {}
    todo = list(range(len(jobs)))
    t = 0
    while todo:
        ports = sorted(set((jobs[i]["src"], jobs[i]["die"]) for i in todo), key=lambda p: (-rem_out[p], p))
        for p in ports:
            if outf.get(p, 0) > t:
                continue
            best, bkey = None, None
            for i in todo:
                j = jobs[i]
                if (j["src"], j["die"]) != p or j["avail"] is None or j["avail"] > t:
                    continue
                q = (j["dst"], j["die"])
                if inf.get(q, 0) > t:
                    continue
                key = (-len(j["kids"]), -rem_in[q], i)
                if best is None or key < bkey:
                    best, bkey = i, key
            if best is None:
                continue
            j = jobs[best]
            q = (j["dst"], j["die"])
            j["start"] = t
            outf[p] = t + j["ln"]
            inf[q] = t + j["ln"]
            rem_out[p] -= j["ln"]
            rem_in[q] -= j["ln"]
            for k in j["kids"]:
                jobs[k]["avail"] = t + j["ln"] + lag
            todo.remove(best)
        t += 1


def make_plan(wid, cores, topo, opt):
    n = len(wid)
    off = [sum(wid[:r]) for r in range(n)]
    chip_of = [topo.chip(c) for c in cores]
    rcore = dict((chip_of[r], cores[r]) for r in range(n))
    lag = opt["lag"]

    cells, groups = [], []
    ncell = {}
    for r, w in enumerate(wid):
        if w % CW:
            ncell[chip_of[r]] = 0
            groups.append({"rank": r, "cells": [], "die": None})
            continue
        k = w // CW
        rows = 128 // k
        ids = []
        for i in range(k):
            ids.append(len(cells))
            cells.append((r, i * rows, (i + 1) * rows))
        ncell[chip_of[r]] = k
        if k == 1:
            groups.append({"rank": r, "cells": ids, "die": None})
        else:
            groups.append({"rank": r, "cells": ids[:k // 2], "die": 1})
            groups.append({"rank": r, "cells": ids[k // 2:], "die": 0})
    for i, gr in enumerate(groups):
        gr["gid"] = i
        gr["chip"] = chip_of[gr["rank"]]

    jobs = []
    outl, inl = {}, {}

    def add_job(gr, src, dst, die, parent):
        j = {"g": gr["gid"], "src": src, "dst": dst, "die": die, "ln": len(gr["cells"]), "kids": [],
             "avail": 0 if parent is None else None, "parent": parent, "start": None}
        jobs.append(j)
        outl[(src, die)] = outl.get((src, die), 0) + j["ln"]
        inl[(dst, die)] = inl.get((dst, die), 0) + j["ln"]
        if parent is not None:
            jobs[parent]["kids"].append(len(jobs) - 1)
        return len(jobs) - 1

    for par in (0, 1):
        mem = sorted(c for c in chip_of if c % 2 == par)
        load = dict((c, (len(mem) - 1) * ncell[c]) for c in mem)
        for i, a in enumerate(mem):
            rot = [mem[(i + s) % len(mem)] for s in range(1, len(mem))]
            mine = [gr for gr in groups if gr["chip"] == a and gr["die"] is not None]
            if ncell[a] == 4 and opt["nrelay"]:
                via = sorted((c for c in mem if ncell[c] < 4), key=lambda c: (load[c], c))[:opt["nrelay"]]
                rest = [d for d in rot if d not in via]
                far = rest[len(rest) - len(via):]
                for gr in mine:
                    for d in rest[:len(rest) - len(via)]:
                        add_job(gr, a, d, gr["die"], None)
                    for v, d in zip(via, far):
                        p = add_job(gr, a, v, gr["die"], None)
                        add_job(gr, v, d, gr["die"], p)
                for v in via:
                    load[v] += ncell[a]
            else:
                for gr in mine:
                    for d in rot:
                        add_job(gr, a, d, gr["die"], None)
        for i, a in enumerate(mem):
            for gr in groups:
                if gr["chip"] == a and gr["die"] is None and gr["cells"]:
                    for s in range(1, len(mem)):
                        d = mem[(i + s) % len(mem)]
                        cost = [max(outl.get((a, e), 0), inl.get((d, e), 0)) * 100 + outl.get((a, e), 0)
                                + inl.get((d, e), 0) for e in (0, 1)]
                        add_job(gr, a, d, 1 if cost[1] < cost[0] else 0, None)
    list_schedule(jobs, lag)

    prog = {}
    arrive = {}
    sent = {}

    def P(core):
        if core not in prog:
            prog[core] = {"g": [], "sync": [], "scalar": []}
        return prog[core]

    def call(core, transfers, lsem):
        for spec, dsts, mask, gid in transfers:
            cnt = bin(mask).count("1")
            for d in dsts:
                arrive[(d, gid)] = arrive.get((d, gid), 0) + cnt
            sent[(core, lsem)] = sent.get((core, lsem), 0) + cnt
        P(core)["g"].append(("call", transfers, lsem))

    est = {}

    hsend = {}
    for ji, j in enumerate(jobs):
        j["idx"] = ji
    for c in chip_of:
        for die in (0, 1):
            h = [8 * c + (0 if die else 4), 8 * c + (1 if die else 5)]
            mine = sorted((j for j in jobs if j["src"] == c and j["die"] == die and j["parent"] is None),
                          key=lambda j: (j["start"], j["idx"]))
            alt = 0
            for j in mine:
                cs = groups[j["g"]]["cells"]
                if len(cs) == 2:
                    for hh, cell in zip(h, cs):
                        hsend.setdefault(hh, []).append((cell, j))
                else:
                    hsend.setdefault(h[alt], []).append((cs[0], j))
                    alt ^= 1

    node = {}
    mate_jobs = {}
    for c in chip_of:
        arr = sorted((j for j in jobs if j["dst"] == c), key=lambda j: (j["start"] + j["ln"], j["idx"]))
        L = {1: ncell[c], 0: 0}
        die_of = {}
        for j in arr:
            if j["kids"]:
                die_of[j["idx"]] = j["die"]
                L[j["die"]] += j["ln"]
        for j in sorted((j for j in arr if not j["kids"]), key=lambda j: (-j["ln"], j["start"], j["idx"])):
            e = 1 if L[1] < L[0] else 0
            die_of[j["idx"]] = e
            L[e] += j["ln"]
        cnt = {6: 0, 7: 0}
        for j in arr:
            if die_of[j["idx"]] == 1:
                k = 3
            else:
                k = 6 if cnt[6] <= cnt[7] else 7
                cnt[k] += j["ln"]
            node[(c, j["g"])] = 8 * c + k
            mate_jobs.setdefault((c, die_of[j["idx"]]), []).append(j)

    tiny = {}
    for r in range(n):
        c, core, w = chip_of[r], cores[r], wid[r]
        mate = rcore[c ^ 1]
        mine = [gr for gr in groups if gr["rank"] == r]
        if w % CW:
            gr = mine[0]
            P(core)["sync"].append(("dma", ("t", r), ("x", 0, 128, w), "ld"))
            P(core)["g"].append(("wait", "ld", 16))
            same = [d for d in chip_of if d != c and d % 2 == c % 2]
            call(core, [(("t", r), [mate] + [rcore[d] for d in same] + [8 * d + 7 for d in same], eng(0, 8), gr["gid"])], "dl")
            for d in same:
                est[(d, gr["gid"])] = 0.5
                est[(d ^ 1, gr["gid"])] = 3
                tiny.setdefault(d, []).append(gr)
            est[(c ^ 1, gr["gid"])] = 0.5
            continue
        k0 = mine[0]["cells"][0]
        k = w // CW
        P(core)["sync"].append(("dma", ("cbr", k0, k0 + k), ("x", 0, 128, w), "ld"))
        P(core)["g"].append(("wait", "ld", 16))
        gid_of = {}
        for gr in mine:
            for cell in gr["cells"]:
                gid_of[cell] = gr["gid"]
        need = []
        for hh in sorted(hsend):
            if hh // 8 == c:
                for cell in sorted(set(cell for cell, j in hsend[hh])):
                    need.append((cell, hh))
        per = 16
        while per * len(need) > 16:
            per //= 2
        call(core, [(("cb", cell), [hh], eng(i * per, per), gid_of[cell]) for i, (cell, hh) in enumerate(need)], "dl")
        per = 8 // k
        call(core, [(("cb", k0 + i), [mate], eng(i * per, per), gid_of[k0 + i]) for i in range(k)], "sent")
        for gr in mine:
            est[(c ^ 1, gr["gid"])] = 0.25 * k

    for hh in sorted(hsend):
        lst = hsend[hh]
        seen = []
        for cell, j in lst:
            if j["g"] not in seen:
                seen.append(j["g"])
        for gid in seen:
            P(hh)["g"].append(("waitg", gid))
        for cell, j in lst:
            call(hh, [(("cb", cell), [node[(j["dst"], j["g"])]], eng(0, 8), j["g"])], "sent")

    for d in sorted(tiny):
        per = 8 // len(tiny[d])
        for gr in tiny[d]:
            P(8 * d + 7)["g"].append(("waitg", gr["gid"]))
        call(8 * d + 7, [(("t", gr["rank"]), [rcore[d ^ 1]], eng(i * per, per), gr["gid"]) for i, gr in enumerate(tiny[d])], "sent")

    acts = {}
    for (c, die), lst in sorted(mate_jobs.items()):
        free = ncell[c] if die == 1 else 0
        for j in sorted(lst, key=lambda j: (j["start"] + j["ln"], j["idx"])):
            a = j["start"] + j["ln"]
            free = max(free, a + lag) + j["ln"]
            est[(c ^ 1, j["g"])] = free
            est[(c, j["g"])] = a + lag + 0.5 * j["ln"]
            acts.setdefault(node[(c, j["g"])], []).append(j)
    for nd in sorted(acts):
        c = nd // 8
        for j in sorted(acts[nd], key=lambda j: (j["start"] + j["ln"], j["idx"])):
            cl = groups[j["g"]]["cells"]
            per = 8 // len(cl)
            tr = []
            if j["kids"]:
                hp = per // 2
                for i, cell in enumerate(cl):
                    tr.append((("cb", cell), [node[(jobs[k]["dst"], j["g"])] for k in j["kids"]], eng(i * hp, hp), j["g"]))
                    tr.append((("cb", cell), [rcore[c ^ 1]], eng(4 + i * hp, hp), j["g"]))
            else:
                for i, cell in enumerate(cl):
                    tr.append((("cb", cell), [rcore[c ^ 1]], eng(i * per, per), j["g"]))
            for i, cell in enumerate(cl):
                tr.append((("cb", cell), [rcore[c]], eng(8 + i * per, per), j["g"]))
            P(nd)["g"].append(("waitg", j["g"]))
            call(nd, tr, "sent")

    for r in range(n):
        c, core, w = chip_of[r], cores[r], wid[r]
        pr = P(core)
        pr["scalar"].append(("wait", "dl", sent[(core, "dl")]))
        pr["scalar"].append(("dma", ("y", 0, 128, off[r], off[r] + w), ("x", 0, 128, w), "ssc"))
        cnt = {"sync": 0, "scalar": 1}
        todo = sorted((gr for gr in groups if gr["rank"] != r), key=lambda gr: (est[(c, gr["gid"])], gr["gid"]))
        for i, gr in enumerate(todo):
            q = "sync" if i % 2 == 0 else "scalar"
            o, ww = off[gr["rank"]], wid[gr["rank"]]
            pr[q].append(("waitg", gr["gid"]))
            if gr["cells"]:
                k0, k1 = gr["cells"][0], gr["cells"][-1]
                src = ("cb", k0) if k0 == k1 else ("cbr", k0, k1 + 1)
                pr[q].append(("dma", ("y", cells[k0][1], cells[k1][2], o, o + ww), src, "ssy" if q == "sync" else "ssc"))
            else:
                pr[q].append(("dma", ("y", 0, 128, o, o + ww), ("t", gr["rank"]), "ssy" if q == "sync" else "ssc"))
            cnt[q] += 1
        pr["sync"].append(("wait", "ssy", 16 * cnt["sync"]))
        pr["scalar"].append(("wait", "ssc", 16 * cnt["scalar"]))

    for core in prog:
        if (core, "sent") in sent:
            prog[core]["g"].append(("wait", "sent", sent[(core, "sent")]))
        for q in prog[core]:
            prog[core][q] = [("wait", "a%d" % op[1], arrive[(core, op[1])]) if op[0] == "waitg" else op
                             for op in prog[core][q]]
    return {"prog": prog, "jobs": jobs, "groups": groups, "node": node, "est": est}


def rank_program(g, core, T, topo):
    if "plan" not in CACHE:
        CACHE["plan"] = make_plan(list(T.tables["WIDTHS"]), list(T.cores), topo, OPT)
    ops = CACHE["plan"]["prog"].get(core)
    if not ops:
        return

    def ap(s):
        if s[0] == "cb":
            return T.cb[s[1]]
        if s[0] == "cbr":
            return T.cb[s[1]:s[2]]
        if s[0] == "t":
            return T["t%d" % s[1]][:]
        if s[0] == "x":
            return T.x[s[1]:s[2], 0:s[3]]
        return T.y[s[1]:s[2], s[3]:s[4]]

    for qn, q in (("sync", g.sync), ("scalar", g.scalar), ("g", g)):
        for op in ops[qn]:
            if op[0] == "wait":
                q.wait_ge(T.sem[op[1]], op[2])
            elif op[0] == "dma":
                q.dma_start(ap(op[1]), ap(op[2])).then_inc(T.sem[op[3]], 16)
            else:
                trs, lsem = op[1], op[2]
                if len(trs) == 1 and len(trs[0][1]) == 1:
                    spec, dsts, mask, gid = trs[0]
                    rid, pid, se = topo.addr(dsts[0])
                    g.remote_dma(ap(spec), ap(spec), T.sem["a%d" % gid], T.sem[lsem], pid, rid, mask)
                else:
                    lst = []
                    for spec, dsts, mask, gid in trs:
                        ids = [DstId(rid=topo.addr(d)[0], pnc=topo.addr(d)[1]) for d in dsts]
                        lst.append(RemoteDMATransfer(dst_ids=ids, dma_engine_mask=mask, remote_sem=T.sem["a%d" % gid],
                                                     srcs=[ap(spec)], dsts=[ap(spec) for d in dsts], alu_op=0))
                    g.remote_dma_fused(lst, local_sem=T.sem[lsem])
